import numpy as np
import ml_dtypes


def mxq(x, axis, fmt="e4m3"):
    dtype, down = {"e4m3": (ml_dtypes.float8_e4m3fn, 7), "e5m2": (ml_dtypes.float8_e5m2, 14)}[fmt]
    v = np.moveaxis(np.asarray(x, np.float32).astype(ml_dtypes.bfloat16).astype(np.float64), axis, -1)
    blocks = v.reshape(v.shape[:-1] + (-1, 32))
    amax = np.abs(blocks).max(-1, keepdims=True)
    byte = np.maximum(np.where(amax > 0, np.frexp(amax)[1] - 1 + 127, 0) - down, 1)
    scale = np.exp2(byte - 127.0)
    codes = (blocks / scale).astype(np.float32).astype(dtype).astype(np.float64)
    return np.moveaxis((codes * scale).reshape(v.shape), -1, axis)


WIDE = False


def mx_kscale(k):
    if not WIDE:
        return np.ones(k)
    levels = np.array([10, -10, 5, -5, 0])
    if k % 512:
        return np.exp2(np.random.permutation(np.resize(levels, k // 32))).repeat(32)
    a = np.empty((k // 512, 16))
    for p in range(k // 512):
        a[p, :8] = np.random.permutation(np.resize(levels, 8))
        for g in range(8):
            far = levels[np.abs(levels - a[p, g]) >= 10]
            a[p, g + 8] = far[np.random.randint(len(far))]
    return np.exp2(a.ravel()).repeat(32)


def f64(x):
    return np.asarray(x).astype(np.float64)


def striped(idx):
    return np.tile(idx.reshape(-1, 16).T, (8, 1)).astype(np.uint16)


def unstriped(offs):
    return offs[:16].T.reshape(-1).astype(np.int64)


def pack_weight(w):
    k, n = w.shape
    w = f64(np.asarray(w, np.float32).astype(ml_dtypes.bfloat16)).reshape(k // 32, 32, n)
    amax = np.abs(w).max(1)
    byte = np.clip(np.where(amax > 0, np.frexp(amax)[1] - 1 + 127 - 7, 1), 1, 254)
    scaled = (w * np.exp2(127.0 - byte)[:, None, :]).reshape(k, n).astype(np.float32)
    words = np.ascontiguousarray(scaled.reshape(k // 512, 128, 4, n).transpose(0, 1, 3, 2)).astype(ml_dtypes.float8_e4m3fn).view(np.uint8)
    return words, np.ascontiguousarray(byte.astype(np.uint8).reshape(k // 512, 16, n))


def unpack_weight(words, scales):
    g, p, n, _ = words.shape
    vals = np.ascontiguousarray(words).view(ml_dtypes.float8_e4m3fn).astype(np.float64) * np.repeat(np.exp2(scales.astype(np.float64) - 127.0), 8, axis=1)[..., None]
    return vals.transpose(0, 1, 3, 2).reshape(g * 512, n)


def gelu(v):
    return 0.5 * v * (1.0 + np.tanh(np.sqrt(2.0 / np.pi) * (v + 0.044715 * v**3)))


K, T, D, S, V, N = 1024, 2048, 4, 768, 384, 256


def setup_inputs():
    n = np.random.standard_normal
    s = mx_kscale(K)[:, None]
    words, scales = pack_weight(n((K, N)) / np.sqrt(K) / s)
    return {
        "xT": (n((K, T)) * s).astype(np.float32),
        "w_words": words,
        "w_scales": scales,
        "b": (0.3 * n((N, 1))).astype(np.float32),
        "gate": np.tile(np.random.uniform(0.2, 1.0, (D, 1, V)) / np.sqrt(D), (1, N, 1)).astype(np.float32),
        "offs": striped(np.random.permutation(T)[:S]),
        "pos1": striped(np.random.permutation(S)[:V]),
        "pos2": striped(np.random.permutation(S)[:V]),
        "pos3": striped(np.random.permutation(S)[:V]),
        "pos4": striped(np.random.permutation(S)[:V]),
    }


def reference(xT, w_words, w_scales, b, gate, offs, pos1, pos2, pos3, pos4):
    w = unpack_weight(w_words, w_scales)
    idx = unstriped(offs)
    xq = mxq(f64(xT)[:, idx], 0, "e4m3")
    y = w.T @ xq
    y = gelu(y + f64(b))
    return sum(f64(gate[d]) * y[:, unstriped(p)] for d, p in enumerate((pos1, pos2, pos3, pos4)))

@@ -1,0 +1,185 @@
+from contextlib import ExitStack
+
+import concourse.mybir as mybir
+
+K, T, D, S, V, N = 1024, 2048, 4, 768, 384, 256
+FLOPS = 2 * K * S * N
+
+F32 = mybir.dt.float32
+BF16 = mybir.dt.bfloat16
+I32 = mybir.dt.int32
+U32 = mybir.dt.uint32
+U16 = mybir.dt.uint16
+U8 = mybir.dt.uint8
+FP8X4 = mybir.dt.float8_e4m3fn_x4
+GELU = mybir.ActivationFunctionType.Gelu_apprx_tanh
+MULT = mybir.AluOpType.mult
+ADD = mybir.AluOpType.add
+
+P = 128
+PACK = 4
+K_PASS = P * PACK
+PASSES = K // K_PASS
+BLOCKS = N // P
+W = 256
+PIECES = S // W
+LANES = 16
+
+
+def tile_picked_sub_lin_gelu_sub_e_kernel(
+    tc, xT, w_words, w_scales, b, gate, offs, pos1, pos2, pos3, pos4, out
+):
+    nc = tc.nc
+    with ExitStack() as ctx:
+        lists = ctx.enter_context(tc.tile_pool(name="lists", bufs=1))
+        keep = ctx.enter_context(tc.tile_pool(name="keep", bufs=1))
+        psum = ctx.enter_context(tc.psum_pool(name="psum", bufs=1))
+
+        warm_in = keep.tile([P, 1], F32, name="warm_in")
+        warm_out = keep.tile([P, 1], F32, name="warm_out")
+        nc.vector.memset(warm_in[:], 0.0)
+        nc.scalar.activation(warm_out[:], warm_in[:], GELU)
+
+        w_sc = keep.tile([P, PASSES, N], U8, name="w_sc", align_bytes=64)
+        nc.gpsimd.memset(w_sc[:].bitcast(I32), 0)
+        for q in range(4):
+            nc.gpsimd.dma_start(
+                out=w_sc[32 * q : 32 * q + 4].bitcast(I32),
+                in_=w_scales[:, 4 * q : 4 * q + 4, :].rearrange("a r n -> r a n").bitcast(I32),
+            )
+        bias = keep.tile([P, BLOCKS], F32, name="bias")
+        with nc.allow_non_contiguous_dma(reason="one bias value to a partition"):
+            nc.gpsimd.dma_start(out=bias[:], in_=b.rearrange("(c p) o -> p (c o)", p=P))
+
+        picks = lists.tile([P, S // LANES], U16, name="picks")
+        planes = []
+        for a in range(PASSES):
+            rows = xT[a * K_PASS : (a + 1) * K_PASS, :].rearrange("(p t) w -> p t w", t=PACK)
+            for t in range(PACK):
+                plane = keep.tile([P, T], F32, name="plane%d%d" % (a, t))
+                nc.sync.dma_start(out=plane[:], in_=rows[:, t, :])
+                planes.append(plane)
+                if len(planes) == 1:
+                    nc.sync.dma_start(picks[:], offs)
+        w_cd = keep.tile([P, PASSES, N], U32, name="w_cd", align_bytes=64)
+        nc.sync.dma_start(
+            out=w_cd[:].bitcast(I32), in_=w_words.rearrange("a p n t -> p a (n t)").bitcast(I32)
+        )
+        nbrs = []
+        for d, pos in enumerate((pos1, pos2, pos3, pos4)):
+            nbr = lists.tile([P, V // LANES], U16, name="nbr%d" % d)
+            nc.sync.dma_start(nbr[:], pos)
+            nbrs.append(nbr)
+        gates = []
+        for m in range(BLOCKS):
+            g = keep.tile([P, D, V], F32, name="gate%d" % m)
+            nc.sync.dma_start(out=g[:], in_=gate[:, m * P : (m + 1) * P, :].rearrange("d p v -> p d v"))
+            gates.append(g)
+
+        picked = [keep.tile([P, PACK, S], F32, name="picked%d" % a) for a in range(PASSES)]
+        grouped = [keep.tile([P, S, PACK], BF16, name="grouped%d" % a, align_bytes=64) for a in range(PASSES)]
+        x_cd = [keep.tile([P, S], U32, name="x_cd%d" % a, align_bytes=64) for a in range(PASSES)]
+        x_sc = [keep.tile([P, S], U8, name="x_sc%d" % a, align_bytes=64) for a in range(PASSES)]
+
+        def window(a, t, c0, c1):
+            return planes[PACK * a + t][:].indirect(picks[:, c0 // LANES : c1 // LANES])
+
+        def gather(a, t, c0, c1):
+            nc.vector.tensor_copy(picked[a][:, t, c0:c1], window(a, t, c0, c1))
+
+        def gather_rounded(a, t, c0, c1):
+            nc.vector.tensor_copy(grouped[a][:, c0:c1, t], window(a, t, c0, c1))
+
+        def round_pair(a, t, c0, c1):
+            nc.scalar.copy(
+                grouped[a][:, c0:c1, t : t + 2],
+                picked[a][:, t : t + 2, c0:c1].rearrange("p t n -> p n t"),
+            )
+
+        def quantize(a, c0, c1):
+            nc.vector.quantize_mx(
+                out=x_cd[a][:, c0:c1].bitcast(FP8X4),
+                scales=x_sc[a][:, c0:c1],
+                in_=grouped[a][:, c0:c1, :].rearrange("p n t -> p (n t)"),
+            )
+
+        gather(0, 0, 0, S)
+        gather(0, 1, 0, S)
+        round_pair(0, 0, 0, S)
+        gather(0, 2, 0, S)
+        gather(0, 3, 0, S)
+        round_pair(0, 2, 0, 2 * W)
+        round_pair(0, 2, 2 * W, S)
+        gather(1, 0, 0, S)
+        quantize(0, 0, 2 * W)
+        quantize(0, 2 * W, S)
+        gather(1, 1, 0, S)
+        round_pair(1, 0, 0, S)
+        gather(1, 2, 0, 2 * W)
+        gather_rounded(1, 2, 2 * W, S)
+        for j in range(PIECES - 1):
+            gather(1, 3, j * W, (j + 1) * W)
+            round_pair(1, 2, j * W, (j + 1) * W)
+        gather_rounded(1, 3, 2 * W, S)
+        for j in range(PIECES):
+            quantize(1, j * W, (j + 1) * W)
+
+        acc = [[psum.tile([P, W], F32, name="acc%d%d" % (m, j)) for j in range(PIECES)] for m in range(BLOCKS)]
+        ys = [keep.tile([P, S], F32, name="y%d" % m) for m in range(BLOCKS)]
+
+        def multiply(m, j, a):
+            nc.tensor.matmul_mx(
+                out=acc[m][j][:],
+                lhsT=w_cd[:, a, m * P : (m + 1) * P].bitcast(FP8X4),
+                lhsT_scale=w_sc[:, a, m * P : (m + 1) * P],
+                rhs=x_cd[a][:, j * W : (j + 1) * W].bitcast(FP8X4),
+                rhs_scale=x_sc[a][:, j * W : (j + 1) * W],
+                start=(a == 0),
+                stop=(a == PASSES - 1),
+            )
+
+        for m in range(BLOCKS):
+            for a in range(PASSES):
+                for j in range(PIECES):
+                    multiply(m, j, a)
+            for j in range(PIECES):
+                nc.scalar.activation(ys[m][:, j * W : (j + 1) * W], acc[m][j][:], GELU, bias=bias[:, m : m + 1])
+
+        terms = [[keep.tile([P, V], F32, name="term%d%d" % (m, d)) for d in range(D)] for m in range(BLOCKS)]
+        sums = [[keep.tile([P, V], F32, name="sum%d%d" % (m, d)) for d in range(D - 1)] for m in range(BLOCKS)]
+
+        def fetch(m, d, c0, c1):
+            nc.vector.tensor_tensor(
+                terms[m][d][:, c0:c1],
+                ys[m][:].indirect(nbrs[d][:, c0 // LANES : c1 // LANES]),
+                gates[m][:, d, c0:c1],
+                MULT,
+            )
+
+        def add(m, d, c0, c1):
+            left = terms[m][0] if d == 1 else sums[m][d - 2]
+            nc.vector.tensor_tensor(sums[m][d - 1][:, c0:c1], left[:, c0:c1], terms[m][d][:, c0:c1], ADD)
+
+        def store(m, c0, c1):
+            nc.sync.dma_start(out=out[m * P : (m + 1) * P, c0:c1], in_=sums[m][D - 2][:, c0:c1])
+
+        H = V // 2
+        fetch(0, 0, 0, V)
+        fetch(0, 1, 0, V)
+        fetch(0, 2, 0, V)
+        add(0, 1, 0, V)
+        fetch(0, 3, 0, V)
+        add(0, 2, 0, V)
+        fetch(1, 0, 0, V)
+        add(0, 3, 0, V)
+        store(0, 0, V)
+        fetch(1, 1, 0, V)
+        fetch(1, 2, 0, V)
+        add(1, 1, 0, V)
+        fetch(1, 3, 0, H)
+        add(1, 2, 0, V)
+        fetch(1, 3, H, V)
+        add(1, 3, 0, H)
+        store(1, 0, H)
+        add(1, 3, H, V)
+        store(1, H, V)

@@ -1,6 +1,7 @@
 from contextlib import ExitStack
 
 import concourse.mybir as mybir
+from concourse.masks import make_identity
 
 K, T, D, S, V, N = 1024, 2048, 4, 768, 384, 256
 FLOPS = 2 * K * S * N
@@ -41,22 +42,25 @@ def tile_picked_sub_lin_gelu_sub_e_kernel(
         nc.scalar.activation(warm_out[:], warm_in[:], GELU)
 
         w_sc = keep.tile([P, PASSES, N], U8, name="w_sc", align_bytes=64)
-        nc.gpsimd.memset(w_sc[:].bitcast(I32), 0)
+        nc.vector.memset(w_sc[:].bitcast(I32), 0)
         for q in range(4):
-            nc.gpsimd.dma_start(
+            nc.scalar.dma_start(
                 out=w_sc[32 * q : 32 * q + 4].bitcast(I32),
                 in_=w_scales[:, 4 * q : 4 * q + 4, :].rearrange("a r n -> r a n").bitcast(I32),
             )
         bias = keep.tile([P, BLOCKS], F32, name="bias")
         with nc.allow_non_contiguous_dma(reason="one bias value to a partition"):
-            nc.gpsimd.dma_start(out=bias[:], in_=b.rearrange("(c p) o -> p (c o)", p=P))
+            nc.scalar.dma_start(out=bias[:], in_=b.rearrange("(c p) o -> p (c o)", p=P))
+
+        ident = keep.tile([P, P], F32, name="ident")
+        make_identity(nc, ident[:])
 
         picks = lists.tile([P, S // LANES], U16, name="picks")
         planes = []
         for a in range(PASSES):
             rows = xT[a * K_PASS : (a + 1) * K_PASS, :].rearrange("(p t) w -> p t w", t=PACK)
             for t in range(PACK):
-                plane = keep.tile([P, T], F32, name="plane%d%d" % (a, t))
+                plane = keep.tile([P, T], F32, name="plane%d%d" % (a, t), align_bytes=64)
                 nc.sync.dma_start(out=plane[:], in_=rows[:, t, :])
                 planes.append(plane)
                 if len(planes) == 1:
@@ -76,110 +80,153 @@ def tile_picked_sub_lin_gelu_sub_e_kernel(
             nc.sync.dma_start(out=g[:], in_=gate[:, m * P : (m + 1) * P, :].rearrange("d p v -> p d v"))
             gates.append(g)
 
-        picked = [keep.tile([P, PACK, S], F32, name="picked%d" % a) for a in range(PASSES)]
         grouped = [keep.tile([P, S, PACK], BF16, name="grouped%d" % a, align_bytes=64) for a in range(PASSES)]
-        x_cd = [keep.tile([P, S], U32, name="x_cd%d" % a, align_bytes=64) for a in range(PASSES)]
         x_sc = [keep.tile([P, S], U8, name="x_sc%d" % a, align_bytes=64) for a in range(PASSES)]
+        x_cd = {}
 
         def window(a, t, c0, c1):
             return planes[PACK * a + t][:].indirect(picks[:, c0 // LANES : c1 // LANES])
 
-        def gather(a, t, c0, c1):
-            nc.vector.tensor_copy(picked[a][:, t, c0:c1], window(a, t, c0, c1))
+        def pair_tile(name, width):
+            return keep.tile([P, 2, width], F32, name=name, align_bytes=64)
+
+        def gather(pair, a, t, c0, c1):
+            nc.vector.tensor_copy(pair[:, t % 2, :], window(a, t, c0, c1))
 
         def gather_rounded(a, t, c0, c1):
             nc.vector.tensor_copy(grouped[a][:, c0:c1, t], window(a, t, c0, c1))
 
-        def round_pair(a, t, c0, c1):
-            nc.scalar.copy(
-                grouped[a][:, c0:c1, t : t + 2],
-                picked[a][:, t : t + 2, c0:c1].rearrange("p t n -> p n t"),
-            )
+        def round_pair(pair, a, t, c0, c1):
+            nc.scalar.copy(grouped[a][:, c0:c1, t : t + 2], pair.rearrange("p t n -> p n t"))
 
-        def quantize(a, c0, c1):
+        def quantize(a, c0, c1, tag):
+            codes = keep.tile([P, c1 - c0], U32, name="x_cd%d_%d" % (a, c0), tag=tag, align_bytes=64)
             nc.vector.quantize_mx(
-                out=x_cd[a][:, c0:c1].bitcast(FP8X4),
+                out=codes[:].bitcast(FP8X4),
                 scales=x_sc[a][:, c0:c1],
                 in_=grouped[a][:, c0:c1, :].rearrange("p n t -> p (n t)"),
             )
+            for c in range(c0, c1, W):
+                x_cd[a, c // W] = codes[:, c - c0 : c - c0 + W]
 
-        gather(0, 0, 0, S)
-        gather(0, 1, 0, S)
-        round_pair(0, 0, 0, S)
-        gather(0, 2, 0, S)
-        gather(0, 3, 0, S)
-        round_pair(0, 2, 0, 2 * W)
-        round_pair(0, 2, 2 * W, S)
-        gather(1, 0, 0, S)
-        quantize(0, 0, 2 * W)
-        quantize(0, 2 * W, S)
-        gather(1, 1, 0, S)
-        round_pair(1, 0, 0, S)
-        gather(1, 2, 0, 2 * W)
+        pair00 = pair_tile("pair00", S)
+        gather(pair00, 0, 0, 0, S)
+        gather(pair00, 0, 1, 0, S)
+        round_pair(pair00[:], 0, 0, 0, S)
+        pair02 = pair_tile("pair02", S)
+        gather(pair02, 0, 2, 0, S)
+        gather(pair02, 0, 3, 0, S)
+        round_pair(pair02[:, :, 0 : 2 * W], 0, 2, 0, 2 * W)
+        round_pair(pair02[:, :, 2 * W : S], 0, 2, 2 * W, S)
+        pair10 = pair_tile("pair10", S)
+        gather(pair10, 1, 0, 0, S)
+        quantize(0, 0, 2 * W, "plane10")
+        gather(pair10, 1, 1, 0, S)
+        round_pair(pair10[:], 1, 0, 0, S)
+        quantize(0, 2 * W, S, "plane11")
+        last = [pair_tile("pair12_%d" % j, W) for j in range(PIECES - 1)]
+        for j in range(PIECES - 1):
+            gather(last[j], 1, 2, j * W, (j + 1) * W)
         gather_rounded(1, 2, 2 * W, S)
         for j in range(PIECES - 1):
-            gather(1, 3, j * W, (j + 1) * W)
-            round_pair(1, 2, j * W, (j + 1) * W)
+            gather(last[j], 1, 3, j * W, (j + 1) * W)
+            if j == 0:
+                round_pair(last[j][:], 1, 2, 0, W)
+            else:
+                round_pair(last[j][:, :, 0:P], 1, 2, W, W + P)
+                round_pair(last[j][:, :, P:W], 1, 2, W + P, 2 * W)
         gather_rounded(1, 3, 2 * W, S)
-        for j in range(PIECES):
-            quantize(1, j * W, (j + 1) * W)
+        quantize(1, 0, W, "x_cd1_0")
+        quantize(1, 2 * W, S, "pair12_0")
+        codes = keep.tile([P, W], U32, name="x_cd1_1", align_bytes=64)
+        x_cd[1, 1] = codes[:]
+        for c in range(0, W, P):
+            nc.vector.quantize_mx(
+                out=codes[:, c : c + P].bitcast(FP8X4),
+                scales=x_sc[1][:, W + c : W + c + P],
+                in_=grouped[1][:, W + c : W + c + P, :].rearrange("p n t -> p (n t)"),
+            )
 
-        acc = [[psum.tile([P, W], F32, name="acc%d%d" % (m, j)) for j in range(PIECES)] for m in range(BLOCKS)]
         ys = [keep.tile([P, S], F32, name="y%d" % m) for m in range(BLOCKS)]
 
-        def multiply(m, j, a):
+        def multiply(acc, m, c0, c1, a):
+            j = c0 // W
             nc.tensor.matmul_mx(
-                out=acc[m][j][:],
+                out=acc,
                 lhsT=w_cd[:, a, m * P : (m + 1) * P].bitcast(FP8X4),
                 lhsT_scale=w_sc[:, a, m * P : (m + 1) * P],
-                rhs=x_cd[a][:, j * W : (j + 1) * W].bitcast(FP8X4),
-                rhs_scale=x_sc[a][:, j * W : (j + 1) * W],
+                rhs=x_cd[a, j][:, c0 - j * W : c1 - j * W].bitcast(FP8X4),
+                rhs_scale=x_sc[a][:, c0:c1],
                 start=(a == 0),
                 stop=(a == PASSES - 1),
             )
 
-        for m in range(BLOCKS):
-            for a in range(PASSES):
-                for j in range(PIECES):
-                    multiply(m, j, a)
-            for j in range(PIECES):
-                nc.scalar.activation(ys[m][:, j * W : (j + 1) * W], acc[m][j][:], GELU, bias=bias[:, m : m + 1])
+        def activate(acc, m, c0, c1):
+            nc.scalar.activation(ys[m][:, c0:c1], acc, GELU, bias=bias[:, m : m + 1])
 
-        terms = [[keep.tile([P, V], F32, name="term%d%d" % (m, d)) for d in range(D)] for m in range(BLOCKS)]
-        sums = [[keep.tile([P, V], F32, name="sum%d%d" % (m, d)) for d in range(D - 1)] for m in range(BLOCKS)]
+        spans = [(0, W), (2 * W, S), (W, W + P), (W + P, 2 * W)]
+        acc0 = [psum.tile([P, 2 * W], F32, name="acc%d" % j) for j in range(len(spans))]
+        for a in range(PASSES):
+            for acc, (c0, c1) in zip(acc0, spans):
+                multiply(acc[:, 0 : c1 - c0], 0, c0, c1, a)
+        for acc, (c0, c1) in zip(acc0, spans):
+            activate(acc[:, 0 : c1 - c0], 0, c0, c1)
+        single = psum.tile([P, 2 * W], F32, name="single", tag="acc2")
+        for a in range(PASSES):
+            multiply(single[:, 0:W], 1, 2 * W, S, a)
+        activate(single[:, 0:W], 1, 2 * W, S)
+        double = psum.tile([P, 2 * W], F32, name="double", tag="acc3")
+        for c in (0, W):
+            for a in range(PASSES):
+                multiply(double[:, c : c + W], 1, c, c + W, a)
+        activate(double[:], 1, 0, 2 * W)
+
+        terms = {}
+        turned = [keep.tile([P, V], F32, name="turned%d" % m) for m in range(BLOCKS)]
+        result = [keep.tile([P, V], F32, name="result%d" % m) for m in range(BLOCKS)]
+
+        def term(m, d, tag):
+            terms[m, d] = keep.tile([P, V], F32, name="term%d%d" % (m, d), tag=tag)
 
         def fetch(m, d, c0, c1):
             nc.vector.tensor_tensor(
-                terms[m][d][:, c0:c1],
+                terms[m, d][:, c0:c1],
                 ys[m][:].indirect(nbrs[d][:, c0 // LANES : c1 // LANES]),
                 gates[m][:, d, c0:c1],
                 MULT,
             )
 
-        def add(m, d, c0, c1):
-            left = terms[m][0] if d == 1 else sums[m][d - 2]
-            nc.vector.tensor_tensor(sums[m][d - 1][:, c0:c1], left[:, c0:c1], terms[m][d][:, c0:c1], ADD)
+        def sum_terms(m):
+            across = psum.tile([P, V], F32, name="across%d" % m)
+            for d in range(D - 1):
+                term(m, d, "term%d%d" % (m, d))
+                fetch(m, d, 0, V)
+                for c in range(0, V, P):
+                    nc.tensor.matmul(
+                        across[:, c : c + P],
+                        lhsT=terms[m, d][:, c : c + P],
+                        rhs=ident[:],
+                        is_transpose=True,
+                        start=(d == 0 and c == 0),
+                        stop=(d == D - 2 and c == V - P),
+                    )
+            nc.scalar.copy(turned[m][:], across[:])
+            back = psum.tile([P, V], F32, name="back%d" % m)
+            for c in range(0, V, P):
+                nc.tensor.transpose(back[:, c : c + P], turned[m][:, c : c + P], ident[:])
+            return back
 
-        def store(m, c0, c1):
-            nc.sync.dma_start(out=out[m * P : (m + 1) * P, c0:c1], in_=sums[m][D - 2][:, c0:c1])
+        def finish(m, back, c0, c1):
+            nc.vector.tensor_tensor(result[m][:, c0:c1], back[:, c0:c1], terms[m, D - 1][:, c0:c1], ADD)
+            nc.sync.dma_start(out=out[m * P : (m + 1) * P, c0:c1], in_=result[m][:, c0:c1])
 
-        H = V // 2
-        fetch(0, 0, 0, V)
-        fetch(0, 1, 0, V)
-        fetch(0, 2, 0, V)
-        add(0, 1, 0, V)
-        fetch(0, 3, 0, V)
-        add(0, 2, 0, V)
-        fetch(1, 0, 0, V)
-        add(0, 3, 0, V)
-        store(0, 0, V)
-        fetch(1, 1, 0, V)
-        fetch(1, 2, 0, V)
-        add(1, 1, 0, V)
-        fetch(1, 3, 0, H)
-        add(1, 2, 0, V)
-        fetch(1, 3, H, V)
-        add(1, 3, 0, H)
-        store(1, 0, H)
-        add(1, 3, H, V)
-        store(1, H, V)
+        H = 2 * P
+        backs = [sum_terms(m) for m in range(BLOCKS)]
+        term(0, D - 1, "term10")
+        fetch(0, D - 1, 0, V)
+        term(1, D - 1, "term13")
+        fetch(1, D - 1, 0, H)
+        finish(0, backs[0], 0, V)
+        fetch(1, D - 1, H, V)
+        finish(1, backs[1], 0, H)
+        finish(1, backs[1], H, V)

@@ -43,14 +43,6 @@ def tile_picked_sub_lin_gelu_sub_e_kernel(
 
         w_sc = keep.tile([P, PASSES, N], U8, name="w_sc", align_bytes=64)
         nc.vector.memset(w_sc[:].bitcast(I32), 0)
-        for q in range(4):
-            nc.scalar.dma_start(
-                out=w_sc[32 * q : 32 * q + 4].bitcast(I32),
-                in_=w_scales[:, 4 * q : 4 * q + 4, :].rearrange("a r n -> r a n").bitcast(I32),
-            )
-        bias = keep.tile([P, BLOCKS], F32, name="bias")
-        with nc.allow_non_contiguous_dma(reason="one bias value to a partition"):
-            nc.scalar.dma_start(out=bias[:], in_=b.rearrange("(c p) o -> p (c o)", p=P))
 
         ident = keep.tile([P, P], F32, name="ident")
         make_identity(nc, ident[:])
@@ -65,20 +57,30 @@ def tile_picked_sub_lin_gelu_sub_e_kernel(
                 planes.append(plane)
                 if len(planes) == 1:
                     nc.sync.dma_start(picks[:], offs)
+        for q in range(4):
+            nc.sync.dma_start(
+                out=w_sc[32 * q : 32 * q + 4].bitcast(I32),
+                in_=w_scales[:, 4 * q : 4 * q + 4, :].rearrange("a r n -> r a n").bitcast(I32),
+            )
         w_cd = keep.tile([P, PASSES, N], U32, name="w_cd", align_bytes=64)
         nc.sync.dma_start(
             out=w_cd[:].bitcast(I32), in_=w_words.rearrange("a p n t -> p a (n t)").bitcast(I32)
         )
+        bias = keep.tile([P, BLOCKS], F32, name="bias")
+        with nc.allow_non_contiguous_dma(reason="one bias value to a partition"):
+            nc.sync.dma_start(out=bias[:], in_=b.rearrange("(c p) o -> p (c o)", p=P))
+        gates = [keep.tile([P, D, V], F32, name="gate%d" % m) for m in range(BLOCKS)]
+
+        def load_gate(m):
+            nc.sync.dma_start(out=gates[m][:], in_=gate[:, m * P : (m + 1) * P, :].rearrange("d p v -> p d v"))
+
+        load_gate(0)
         nbrs = []
         for d, pos in enumerate((pos1, pos2, pos3, pos4)):
             nbr = lists.tile([P, V // LANES], U16, name="nbr%d" % d)
             nc.sync.dma_start(nbr[:], pos)
             nbrs.append(nbr)
-        gates = []
-        for m in range(BLOCKS):
-            g = keep.tile([P, D, V], F32, name="gate%d" % m)
-            nc.sync.dma_start(out=g[:], in_=gate[:, m * P : (m + 1) * P, :].rearrange("d p v -> p d v"))
-            gates.append(g)
+        load_gate(1)
 
         grouped = [keep.tile([P, S, PACK], BF16, name="grouped%d" % a, align_bytes=64) for a in range(PASSES)]
         x_sc = [keep.tile([P, S], U8, name="x_sc%d" % a, align_bytes=64) for a in range(PASSES)]
@@ -99,15 +101,23 @@ def tile_picked_sub_lin_gelu_sub_e_kernel(
         def round_pair(pair, a, t, c0, c1):
             nc.scalar.copy(grouped[a][:, c0:c1, t : t + 2], pair.rearrange("p t n -> p n t"))
 
-        def quantize(a, c0, c1, tag):
+        def codes_tile(a, c0, c1, tag):
             codes = keep.tile([P, c1 - c0], U32, name="x_cd%d_%d" % (a, c0), tag=tag, align_bytes=64)
+            for c in range(c0, c1, W):
+                x_cd[a, c // W] = codes[:, c - c0 : c - c0 + W]
+            return codes
+
+        def quantize(codes, a, c0, c1):
             nc.vector.quantize_mx(
-                out=codes[:].bitcast(FP8X4),
+                out=codes.bitcast(FP8X4),
                 scales=x_sc[a][:, c0:c1],
                 in_=grouped[a][:, c0:c1, :].rearrange("p n t -> p (n t)"),
             )
-            for c in range(c0, c1, W):
-                x_cd[a, c // W] = codes[:, c - c0 : c - c0 + W]
+
+        def quantize_after(plane, c0, c1):
+            marker = keep.tile([P, 1], F32, name="marker%d" % c0, align_bytes=64)
+            nc.gpsimd.tensor_copy(marker[:], plane[:, 0:1])
+            quantize(codes_tile(0, c0, c1, "marker%d" % c0)[:], 0, c0, c1)
 
         pair00 = pair_tile("pair00", S)
         gather(pair00, 0, 0, 0, S)
@@ -120,32 +130,26 @@ def tile_picked_sub_lin_gelu_sub_e_kernel(
         round_pair(pair02[:, :, 2 * W : S], 0, 2, 2 * W, S)
         pair10 = pair_tile("pair10", S)
         gather(pair10, 1, 0, 0, S)
-        quantize(0, 0, 2 * W, "plane10")
+        quantize_after(planes[PACK], 0, 2 * W)
         gather(pair10, 1, 1, 0, S)
-        round_pair(pair10[:], 1, 0, 0, S)
-        quantize(0, 2 * W, S, "plane11")
+        quantize_after(planes[PACK + 1], 2 * W, S)
+        round_pair(pair10[:, :, 2 * W : S], 1, 0, 2 * W, S)
+        round_pair(pair10[:, :, 0 : 2 * W], 1, 0, 0, 2 * W)
         last = [pair_tile("pair12_%d" % j, W) for j in range(PIECES - 1)]
         for j in range(PIECES - 1):
             gather(last[j], 1, 2, j * W, (j + 1) * W)
         gather_rounded(1, 2, 2 * W, S)
         for j in range(PIECES - 1):
             gather(last[j], 1, 3, j * W, (j + 1) * W)
-            if j == 0:
-                round_pair(last[j][:], 1, 2, 0, W)
-            else:
-                round_pair(last[j][:, :, 0:P], 1, 2, W, W + P)
-                round_pair(last[j][:, :, P:W], 1, 2, W + P, 2 * W)
+            for c in range(0, W, P):
+                round_pair(last[j][:, :, c : c + P], 1, 2, j * W + c, j * W + c + P)
         gather_rounded(1, 3, 2 * W, S)
-        quantize(1, 0, W, "x_cd1_0")
-        quantize(1, 2 * W, S, "pair12_0")
-        codes = keep.tile([P, W], U32, name="x_cd1_1", align_bytes=64)
-        x_cd[1, 1] = codes[:]
-        for c in range(0, W, P):
-            nc.vector.quantize_mx(
-                out=codes[:, c : c + P].bitcast(FP8X4),
-                scales=x_sc[1][:, W + c : W + c + P],
-                in_=grouped[1][:, W + c : W + c + P, :].rearrange("p n t -> p (n t)"),
-            )
+        spans = []
+        for c0, tag in ((0, "x_cd1_0"), (2 * W, "pair12_0"), (W, "x_cd1_1")):
+            codes = codes_tile(1, c0, c0 + W, tag)
+            for c in range(0, W, P):
+                quantize(codes[:, c : c + P], 1, c0 + c, c0 + c + P)
+                spans.append((c0 + c, c0 + c + P))
 
         ys = [keep.tile([P, S], F32, name="y%d" % m) for m in range(BLOCKS)]
 
@@ -164,18 +168,17 @@ def tile_picked_sub_lin_gelu_sub_e_kernel(
         def activate(acc, m, c0, c1):
             nc.scalar.activation(ys[m][:, c0:c1], acc, GELU, bias=bias[:, m : m + 1])
 
-        spans = [(0, W), (2 * W, S), (W, W + P), (W + P, 2 * W)]
         acc0 = [psum.tile([P, 2 * W], F32, name="acc%d" % j) for j in range(len(spans))]
         for a in range(PASSES):
             for acc, (c0, c1) in zip(acc0, spans):
                 multiply(acc[:, 0 : c1 - c0], 0, c0, c1, a)
         for acc, (c0, c1) in zip(acc0, spans):
             activate(acc[:, 0 : c1 - c0], 0, c0, c1)
-        single = psum.tile([P, 2 * W], F32, name="single", tag="acc2")
+        single = psum.tile([P, 2 * W], F32, name="single", tag="acc4")
         for a in range(PASSES):
             multiply(single[:, 0:W], 1, 2 * W, S, a)
         activate(single[:, 0:W], 1, 2 * W, S)
-        double = psum.tile([P, 2 * W], F32, name="double", tag="acc3")
+        double = psum.tile([P, 2 * W], F32, name="double", tag="acc5")
         for c in (0, W):
             for a in range(PASSES):
                 multiply(double[:, c : c + W], 1, c, c + W, a)
@@ -211,7 +214,7 @@ def tile_picked_sub_lin_gelu_sub_e_kernel(
                         stop=(d == D - 2 and c == V - P),
                     )
             nc.scalar.copy(turned[m][:], across[:])
-            back = psum.tile([P, V], F32, name="back%d" % m)
+            back = psum.tile([P, V], F32, name="back%d" % m, tag="acc%d" % m)
             for c in range(0, V, P):
                 nc.tensor.transpose(back[:, c : c + P], turned[m][:, c : c + P], ident[:])
             return back

@@ -57,30 +57,34 @@ def tile_picked_sub_lin_gelu_sub_e_kernel(
                 planes.append(plane)
                 if len(planes) == 1:
                     nc.sync.dma_start(picks[:], offs)
+        w_cd = keep.tile([P, PASSES, N], U32, name="w_cd", align_bytes=64)
+        nc.sync.dma_start(
+            out=w_cd[:].bitcast(I32), in_=w_words.rearrange("a p n t -> p a (n t)").bitcast(I32)
+        )
         for q in range(4):
             nc.sync.dma_start(
                 out=w_sc[32 * q : 32 * q + 4].bitcast(I32),
                 in_=w_scales[:, 4 * q : 4 * q + 4, :].rearrange("a r n -> r a n").bitcast(I32),
             )
-        w_cd = keep.tile([P, PASSES, N], U32, name="w_cd", align_bytes=64)
-        nc.sync.dma_start(
-            out=w_cd[:].bitcast(I32), in_=w_words.rearrange("a p n t -> p a (n t)").bitcast(I32)
-        )
         bias = keep.tile([P, BLOCKS], F32, name="bias")
         with nc.allow_non_contiguous_dma(reason="one bias value to a partition"):
             nc.sync.dma_start(out=bias[:], in_=b.rearrange("(c p) o -> p (c o)", p=P))
         gates = [keep.tile([P, D, V], F32, name="gate%d" % m) for m in range(BLOCKS)]
+        nbrs = [lists.tile([P, V // LANES], U16, name="nbr%d" % d) for d in range(D)]
 
-        def load_gate(m):
-            nc.sync.dma_start(out=gates[m][:], in_=gate[:, m * P : (m + 1) * P, :].rearrange("d p v -> p d v"))
+        def load_gate(m, d0, d1):
+            nc.sync.dma_start(
+                out=gates[m][:, d0:d1, :],
+                in_=gate[d0:d1, m * P : (m + 1) * P, :].rearrange("d p v -> p d v"),
+            )
 
-        load_gate(0)
-        nbrs = []
-        for d, pos in enumerate((pos1, pos2, pos3, pos4)):
-            nbr = lists.tile([P, V // LANES], U16, name="nbr%d" % d)
-            nc.sync.dma_start(nbr[:], pos)
-            nbrs.append(nbr)
-        load_gate(1)
+        for d, pos in enumerate((pos1, pos2, pos3)):
+            load_gate(0, d, d + 1)
+            nc.sync.dma_start(nbrs[d][:], pos)
+        load_gate(1, 0, D - 1)
+        nc.sync.dma_start(nbrs[D - 1][:], pos4)
+        for m in range(BLOCKS):
+            load_gate(m, D - 1, D)
 
         grouped = [keep.tile([P, S, PACK], BF16, name="grouped%d" % a, align_bytes=64) for a in range(PASSES)]
         x_sc = [keep.tile([P, S], U8, name="x_sc%d" % a, align_bytes=64) for a in range(PASSES)]
@@ -114,9 +118,9 @@ def tile_picked_sub_lin_gelu_sub_e_kernel(
                 in_=grouped[a][:, c0:c1, :].rearrange("p n t -> p (n t)"),
             )
 
-        def quantize_after(plane, c0, c1):
+        def quantize_after(copy, plane, c0, c1):
             marker = keep.tile([P, 1], F32, name="marker%d" % c0, align_bytes=64)
-            nc.gpsimd.tensor_copy(marker[:], plane[:, 0:1])
+            copy(marker[:], plane[:, 0:1])
             quantize(codes_tile(0, c0, c1, "marker%d" % c0)[:], 0, c0, c1)
 
         pair00 = pair_tile("pair00", S)
@@ -130,9 +134,9 @@ def tile_picked_sub_lin_gelu_sub_e_kernel(
         round_pair(pair02[:, :, 2 * W : S], 0, 2, 2 * W, S)
         pair10 = pair_tile("pair10", S)
         gather(pair10, 1, 0, 0, S)
-        quantize_after(planes[PACK], 0, 2 * W)
+        quantize_after(nc.gpsimd.tensor_copy, planes[PACK], 0, 2 * W)
         gather(pair10, 1, 1, 0, S)
-        quantize_after(planes[PACK + 1], 2 * W, S)
+        quantize_after(nc.scalar.copy, planes[PACK + 1], 2 * W, S)
         round_pair(pair10[:, :, 2 * W : S], 1, 0, 2 * W, S)
         round_pair(pair10[:, :, 0 : 2 * W], 1, 0, 0, 2 * W)
         last = [pair_tile("pair12_%d" % j, W) for j in range(PIECES - 1)]
@@ -174,15 +178,11 @@ def tile_picked_sub_lin_gelu_sub_e_kernel(
                 multiply(acc[:, 0 : c1 - c0], 0, c0, c1, a)
         for acc, (c0, c1) in zip(acc0, spans):
             activate(acc[:, 0 : c1 - c0], 0, c0, c1)
-        single = psum.tile([P, 2 * W], F32, name="single", tag="acc4")
-        for a in range(PASSES):
-            multiply(single[:, 0:W], 1, 2 * W, S, a)
-        activate(single[:, 0:W], 1, 2 * W, S)
-        double = psum.tile([P, 2 * W], F32, name="double", tag="acc5")
-        for c in (0, W):
+        for j in range(PIECES):
+            acc = psum.tile([P, 2 * W], F32, name="acc1_%d" % j, tag="acc%d" % (4 + j % 2))
             for a in range(PASSES):
-                multiply(double[:, c : c + W], 1, c, c + W, a)
-        activate(double[:], 1, 0, 2 * W)
+                multiply(acc[:, 0:W], 1, j * W, (j + 1) * W, a)
+            activate(acc[:, 0:W], 1, j * W, (j + 1) * W)
 
         terms = {}
         turned = [keep.tile([P, V], F32, name="turned%d" % m) for m in range(BLOCKS)]
@@ -199,32 +199,40 @@ def tile_picked_sub_lin_gelu_sub_e_kernel(
                 MULT,
             )
 
-        def sum_terms(m):
-            across = psum.tile([P, V], F32, name="across%d" % m)
-            for d in range(D - 1):
-                term(m, d, "term%d%d" % (m, d))
-                fetch(m, d, 0, V)
-                for c in range(0, V, P):
-                    nc.tensor.matmul(
-                        across[:, c : c + P],
-                        lhsT=terms[m, d][:, c : c + P],
-                        rhs=ident[:],
-                        is_transpose=True,
-                        start=(d == 0 and c == 0),
-                        stop=(d == D - 2 and c == V - P),
-                    )
-            nc.scalar.copy(turned[m][:], across[:])
-            back = psum.tile([P, V], F32, name="back%d" % m, tag="acc%d" % m)
+        def turn_and_add(across, m, d, c, start, stop):
+            nc.tensor.matmul(
+                across, lhsT=terms[m, d][:, c : c + P], rhs=ident[:], is_transpose=True, start=start, stop=stop
+            )
+
+        def turn_back(m, tag):
+            back = psum.tile([P, V], F32, name="back%d" % m, tag=tag)
             for c in range(0, V, P):
                 nc.tensor.transpose(back[:, c : c + P], turned[m][:, c : c + P], ident[:])
             return back
+
+        across = psum.tile([P, V], F32, name="across0")
+        for d in range(D - 1):
+            term(0, d, "term0%d" % d)
+            fetch(0, d, 0, V)
+            for c in range(0, V, P):
+                turn_and_add(across[:, c : c + P], 0, d, c, d == 0 and c == 0, d == D - 2 and c == V - P)
+        nc.scalar.copy(turned[0][:], across[:])
+        backs = [turn_back(0, "acc0")]
+        parts = [psum.tile([P, P], F32, name="across1_%d" % i, tag=tag) for i, tag in enumerate(("across1", "acc1", "acc2"))]
+        for d in range(D - 1):
+            term(1, d, "term1%d" % d)
+            fetch(1, d, 0, V)
+            for i in range(V // P):
+                turn_and_add(parts[i][:], 1, d, i * P, d == 0, d == D - 2)
+        for i in range(V // P):
+            nc.scalar.copy(turned[1][:, i * P : (i + 1) * P], parts[i][:])
+        backs.append(turn_back(1, "acc3"))
 
         def finish(m, back, c0, c1):
             nc.vector.tensor_tensor(result[m][:, c0:c1], back[:, c0:c1], terms[m, D - 1][:, c0:c1], ADD)
             nc.sync.dma_start(out=out[m * P : (m + 1) * P, c0:c1], in_=result[m][:, c0:c1])
 
         H = 2 * P
-        backs = [sum_terms(m) for m in range(BLOCKS)]
         term(0, D - 1, "term10")
         fetch(0, D - 1, 0, V)
         term(1, D - 1, "term13")

from contextlib import ExitStack

import concourse.mybir as mybir
from concourse.masks import make_identity

K, T, D, S, V, N = 1024, 2048, 4, 768, 384, 256
FLOPS = 2 * K * S * N

F32 = mybir.dt.float32
BF16 = mybir.dt.bfloat16
I32 = mybir.dt.int32
U32 = mybir.dt.uint32
U16 = mybir.dt.uint16
U8 = mybir.dt.uint8
FP8X4 = mybir.dt.float8_e4m3fn_x4
GELU = mybir.ActivationFunctionType.Gelu_apprx_tanh
MULT = mybir.AluOpType.mult
ADD = mybir.AluOpType.add

P = 128
PACK = 4
K_PASS = P * PACK
PASSES = K // K_PASS
BLOCKS = N // P
W = 256
PIECES = S // W
LANES = 16


def tile_picked_sub_lin_gelu_sub_e_kernel(
    tc, xT, w_words, w_scales, b, gate, offs, pos1, pos2, pos3, pos4, out
):
    nc = tc.nc
    with ExitStack() as ctx:
        lists = ctx.enter_context(tc.tile_pool(name="lists", bufs=1))
        keep = ctx.enter_context(tc.tile_pool(name="keep", bufs=1))
        psum = ctx.enter_context(tc.psum_pool(name="psum", bufs=1))

        warm_in = keep.tile([P, 1], F32, name="warm_in")
        warm_out = keep.tile([P, 1], F32, name="warm_out")
        nc.vector.memset(warm_in[:], 0.0)
        nc.scalar.activation(warm_out[:], warm_in[:], GELU)

        w_sc = keep.tile([P, PASSES, N], U8, name="w_sc", align_bytes=64)
        nc.vector.memset(w_sc[:].bitcast(I32), 0)

        ident = keep.tile([P, P], F32, name="ident")
        make_identity(nc, ident[:])

        picks = lists.tile([P, S // LANES], U16, name="picks")
        planes = []
        for a in range(PASSES):
            rows = xT[a * K_PASS : (a + 1) * K_PASS, :].rearrange("(p t) w -> p t w", t=PACK)
            for t in range(PACK):
                plane = keep.tile([P, T], F32, name="plane%d%d" % (a, t), align_bytes=64)
                nc.sync.dma_start(out=plane[:], in_=rows[:, t, :])
                planes.append(plane)
                if len(planes) == 1:
                    nc.sync.dma_start(picks[:], offs)
        w_cd = keep.tile([P, PASSES, N], U32, name="w_cd", align_bytes=64)
        nc.sync.dma_start(
            out=w_cd[:].bitcast(I32), in_=w_words.rearrange("a p n t -> p a (n t)").bitcast(I32)
        )
        for q in range(4):
            nc.sync.dma_start(
                out=w_sc[32 * q : 32 * q + 4].bitcast(I32),
                in_=w_scales[:, 4 * q : 4 * q + 4, :].rearrange("a r n -> r a n").bitcast(I32),
            )
        bias = keep.tile([P, BLOCKS], F32, name="bias")
        with nc.allow_non_contiguous_dma(reason="one bias value to a partition"):
            nc.sync.dma_start(out=bias[:], in_=b.rearrange("(c p) o -> p (c o)", p=P))
        gates = [keep.tile([P, D, V], F32, name="gate%d" % m) for m in range(BLOCKS)]
        nbrs = [lists.tile([P, V // LANES], U16, name="nbr%d" % d) for d in range(D)]

        def load_gate(m, d0, d1):
            nc.sync.dma_start(
                out=gates[m][:, d0:d1, :],
                in_=gate[d0:d1, m * P : (m + 1) * P, :].rearrange("d p v -> p d v"),
            )

        for d, pos in enumerate((pos1, pos2, pos3)):
            load_gate(0, d, d + 1)
            nc.sync.dma_start(nbrs[d][:], pos)
        load_gate(1, 0, D - 1)
        nc.sync.dma_start(nbrs[D - 1][:], pos4)
        for m in range(BLOCKS):
            load_gate(m, D - 1, D)

        grouped = [keep.tile([P, S, PACK], BF16, name="grouped%d" % a, align_bytes=64) for a in range(PASSES)]
        x_sc = [keep.tile([P, S], U8, name="x_sc%d" % a, align_bytes=64) for a in range(PASSES)]
        x_cd = {}

        def window(a, t, c0, c1):
            return planes[PACK * a + t][:].indirect(picks[:, c0 // LANES : c1 // LANES])

        def pair_tile(name, width):
            return keep.tile([P, 2, width], F32, name=name, align_bytes=64)

        def gather(pair, a, t, c0, c1):
            nc.vector.tensor_copy(pair[:, t % 2, :], window(a, t, c0, c1))

        def gather_rounded(a, t, c0, c1):
            nc.vector.tensor_copy(grouped[a][:, c0:c1, t], window(a, t, c0, c1))

        def round_pair(pair, a, t, c0, c1):
            nc.scalar.copy(grouped[a][:, c0:c1, t : t + 2], pair.rearrange("p t n -> p n t"))

        def codes_tile(a, c0, c1, tag):
            codes = keep.tile([P, c1 - c0], U32, name="x_cd%d_%d" % (a, c0), tag=tag, align_bytes=64)
            for c in range(c0, c1, W):
                x_cd[a, c // W] = codes[:, c - c0 : c - c0 + W]
            return codes

        def quantize(codes, a, c0, c1):
            nc.vector.quantize_mx(
                out=codes.bitcast(FP8X4),
                scales=x_sc[a][:, c0:c1],
                in_=grouped[a][:, c0:c1, :].rearrange("p n t -> p (n t)"),
            )

        def quantize_after(copy, plane, c0, c1):
            marker = keep.tile([P, 1], F32, name="marker%d" % c0, align_bytes=64)
            copy(marker[:], plane[:, 0:1])
            quantize(codes_tile(0, c0, c1, "marker%d" % c0)[:], 0, c0, c1)

        pair00 = pair_tile("pair00", S)
        gather(pair00, 0, 0, 0, S)
        gather(pair00, 0, 1, 0, S)
        round_pair(pair00[:], 0, 0, 0, S)
        pair02 = pair_tile("pair02", S)
        gather(pair02, 0, 2, 0, S)
        gather(pair02, 0, 3, 0, S)
        round_pair(pair02[:, :, 0 : 2 * W], 0, 2, 0, 2 * W)
        round_pair(pair02[:, :, 2 * W : S], 0, 2, 2 * W, S)
        pair10 = pair_tile("pair10", S)
        gather(pair10, 1, 0, 0, S)
        quantize_after(nc.gpsimd.tensor_copy, planes[PACK], 0, 2 * W)
        gather(pair10, 1, 1, 0, S)
        quantize_after(nc.scalar.copy, planes[PACK + 1], 2 * W, S)
        round_pair(pair10[:, :, 2 * W : S], 1, 0, 2 * W, S)
        round_pair(pair10[:, :, 0 : 2 * W], 1, 0, 0, 2 * W)
        last = [pair_tile("pair12_%d" % j, W) for j in range(PIECES - 1)]
        for j in range(PIECES - 1):
            gather(last[j], 1, 2, j * W, (j + 1) * W)
        gather_rounded(1, 2, 2 * W, S)
        for j in range(PIECES - 1):
            gather(last[j], 1, 3, j * W, (j + 1) * W)
            for c in range(0, W, P):
                round_pair(last[j][:, :, c : c + P], 1, 2, j * W + c, j * W + c + P)
        gather_rounded(1, 3, 2 * W, S)
        spans = []
        for c0, tag in ((0, "x_cd1_0"), (2 * W, "pair12_0"), (W, "x_cd1_1")):
            codes = codes_tile(1, c0, c0 + W, tag)
            for c in range(0, W, P):
                quantize(codes[:, c : c + P], 1, c0 + c, c0 + c + P)
                spans.append((c0 + c, c0 + c + P))

        ys = [keep.tile([P, S], F32, name="y%d" % m) for m in range(BLOCKS)]

        def multiply(acc, m, c0, c1, a):
            j = c0 // W
            nc.tensor.matmul_mx(
                out=acc,
                lhsT=w_cd[:, a, m * P : (m + 1) * P].bitcast(FP8X4),
                lhsT_scale=w_sc[:, a, m * P : (m + 1) * P],
                rhs=x_cd[a, j][:, c0 - j * W : c1 - j * W].bitcast(FP8X4),
                rhs_scale=x_sc[a][:, c0:c1],
                start=(a == 0),
                stop=(a == PASSES - 1),
            )

        def activate(acc, m, c0, c1):
            nc.scalar.activation(ys[m][:, c0:c1], acc, GELU, bias=bias[:, m : m + 1])

        acc0 = [psum.tile([P, 2 * W], F32, name="acc%d" % j) for j in range(len(spans))]
        for a in range(PASSES):
            for acc, (c0, c1) in zip(acc0, spans):
                multiply(acc[:, 0 : c1 - c0], 0, c0, c1, a)
        for acc, (c0, c1) in zip(acc0, spans):
            activate(acc[:, 0 : c1 - c0], 0, c0, c1)
        for j in range(PIECES):
            acc = psum.tile([P, 2 * W], F32, name="acc1_%d" % j, tag="acc%d" % (4 + j % 2))
            for a in range(PASSES):
                multiply(acc[:, 0:W], 1, j * W, (j + 1) * W, a)
            activate(acc[:, 0:W], 1, j * W, (j + 1) * W)

        terms = {}
        turned = [keep.tile([P, V], F32, name="turned%d" % m) for m in range(BLOCKS)]
        result = [keep.tile([P, V], F32, name="result%d" % m) for m in range(BLOCKS)]

        def term(m, d, tag):
            terms[m, d] = keep.tile([P, V], F32, name="term%d%d" % (m, d), tag=tag)

        def fetch(m, d, c0, c1):
            nc.vector.tensor_tensor(
                terms[m, d][:, c0:c1],
                ys[m][:].indirect(nbrs[d][:, c0 // LANES : c1 // LANES]),
                gates[m][:, d, c0:c1],
                MULT,
            )

        def turn_and_add(across, m, d, c, start, stop):
            nc.tensor.matmul(
                across, lhsT=terms[m, d][:, c : c + P], rhs=ident[:], is_transpose=True, start=start, stop=stop
            )

        def turn_back(m, tag):
            back = psum.tile([P, V], F32, name="back%d" % m, tag=tag)
            for c in range(0, V, P):
                nc.tensor.transpose(back[:, c : c + P], turned[m][:, c : c + P], ident[:])
            return back

        across = psum.tile([P, V], F32, name="across0")
        for d in range(D - 1):
            term(0, d, "term0%d" % d)
            fetch(0, d, 0, V)
            for c in range(0, V, P):
                turn_and_add(across[:, c : c + P], 0, d, c, d == 0 and c == 0, d == D - 2 and c == V - P)
        nc.scalar.copy(turned[0][:], across[:])
        backs = [turn_back(0, "acc0")]
        parts = [psum.tile([P, P], F32, name="across1_%d" % i, tag=tag) for i, tag in enumerate(("across1", "acc1", "acc2"))]
        for d in range(D - 1):
            term(1, d, "term1%d" % d)
            fetch(1, d, 0, V)
            for i in range(V // P):
                turn_and_add(parts[i][:], 1, d, i * P, d == 0, d == D - 2)
        for i in range(V // P):
            nc.scalar.copy(turned[1][:, i * P : (i + 1) * P], parts[i][:])
        backs.append(turn_back(1, "acc3"))

        def finish(m, back, c0, c1):
            nc.vector.tensor_tensor(result[m][:, c0:c1], back[:, c0:c1], terms[m, D - 1][:, c0:c1], ADD)
            nc.sync.dma_start(out=out[m * P : (m + 1) * P, c0:c1], in_=result[m][:, c0:c1])

        H = 2 * P
        term(0, D - 1, "term10")
        fetch(0, D - 1, 0, V)
        term(1, D - 1, "term13")
        fetch(1, D - 1, 0, H)
        finish(0, backs[0], 0, V)
        fetch(1, D - 1, H, V)
        finish(1, backs[1], 0, H)
        finish(1, backs[1], H, V)
